import numpy as np
import ml_dtypes


def mxq(x, axis, fmt="e4m3"):
    dtype, down = {"e4m3": (ml_dtypes.float8_e4m3fn, 7), "e5m2": (ml_dtypes.float8_e5m2, 14)}[fmt]
    v = np.moveaxis(np.asarray(x, np.float32).astype(ml_dtypes.bfloat16).astype(np.float64), axis, -1)
    blocks = v.reshape(v.shape[:-1] + (-1, 32))
    amax = np.abs(blocks).max(-1, keepdims=True)
    byte = np.maximum(np.where(amax > 0, np.frexp(amax)[1] - 1 + 127, 0) - down, 1)
    scale = np.exp2(byte - 127.0)
    codes = (blocks / scale).astype(np.float32).astype(dtype).astype(np.float64)
    return np.moveaxis((codes * scale).reshape(v.shape), -1, axis)


WIDE = False


def mx_kscale(k):
    if not WIDE:
        return np.ones(k)
    levels = np.array([10, -10, 5, -5, 0])
    if k % 512:
        return np.exp2(np.random.permutation(np.resize(levels, k // 32))).repeat(32)
    a = np.empty((k // 512, 16))
    for p in range(k // 512):
        a[p, :8] = np.random.permutation(np.resize(levels, 8))
        for g in range(8):
            far = levels[np.abs(levels - a[p, g]) >= 10]
            a[p, g + 8] = far[np.random.randint(len(far))]
    return np.exp2(a.ravel()).repeat(32)


def f64(x):
    return np.asarray(x).astype(np.float64)


def striped(idx):
    return np.tile(idx.reshape(-1, 16).T, (8, 1)).astype(np.uint16)


def unstriped(offs):
    return offs[:16].T.reshape(-1).astype(np.int64)


def pack_weight(w):
    k, n = w.shape
    w = f64(np.asarray(w, np.float32).astype(ml_dtypes.bfloat16)).reshape(k // 32, 32, n)
    amax = np.abs(w).max(1)
    byte = np.clip(np.where(amax > 0, np.frexp(amax)[1] - 1 + 127 - 7, 1), 1, 254)
    scaled = (w * np.exp2(127.0 - byte)[:, None, :]).reshape(k, n).astype(np.float32)
    words = np.ascontiguousarray(scaled.reshape(k // 512, 128, 4, n).transpose(0, 1, 3, 2)).astype(ml_dtypes.float8_e4m3fn).view(np.uint8)
    return words, np.ascontiguousarray(byte.astype(np.uint8).reshape(k // 512, 16, n))


def unpack_weight(words, scales):
    g, p, n, _ = words.shape
    vals = np.ascontiguousarray(words).view(ml_dtypes.float8_e4m3fn).astype(np.float64) * np.repeat(np.exp2(scales.astype(np.float64) - 127.0), 8, axis=1)[..., None]
    return vals.transpose(0, 1, 3, 2).reshape(g * 512, n)


def silu(v):
    return v / (1.0 + np.exp(-np.maximum(v, -700.0)))


K, T, S, V, H, N, J = 512, 2048, 1024, 512, 512, 256, 512


def setup_inputs():
    n = np.random.standard_normal
    s = mx_kscale(K)[:, None]
    u = mx_kscale(H)
    r = mx_kscale(J)[:, None]
    packed_w4 = pack_weight(n((H, N)) / np.sqrt(H) / u[:, None])
    return {
        "xT": (n((K, T)) * s).astype(np.float32),
        "eT": (n((J, V)) * r).astype(np.float32),
        "w1": (n((K, H)) / np.sqrt(3 * K) / s * u).astype(np.float32),
        "w2": (n((K, H)) / np.sqrt(3 * K) / s * u).astype(np.float32),
        "w3": (n((J, H)) / np.sqrt(3 * J) / r * u).astype(np.float32),
        "w4_words": packed_w4[0],
        "w4_scales": packed_w4[1],
        "offs": striped(np.random.permutation(T)[:S]),
    }


def reference(xT, eT, w1, w2, w3, w4_words, w4_scales, offs):
    xq = mxq(f64(xT)[:, unstriped(offs)], 0, "e4m3")
    h = silu(mxq(f64(w1), 0, "e4m3").T @ xq[:, :V] + mxq(f64(w2), 0, "e4m3").T @ xq[:, V:2 * V] + mxq(f64(w3), 0, "e4m3").T @ mxq(f64(eT), 0, "e4m3"))
    return unpack_weight(w4_words, w4_scales).T @ mxq(h, 0, "e4m3")

@@ -1,0 +1,174 @@
+from contextlib import ExitStack
+
+import concourse.mybir as mybir
+
+K, T, V, H, N = 512, 2048, 512, 512, 256
+FLOPS = 2 * V * H * (3 * K + N)
+
+F32 = mybir.dt.float32
+BF16 = mybir.dt.bfloat16
+I32 = mybir.dt.int32
+U32 = mybir.dt.uint32
+U16 = mybir.dt.uint16
+U8 = mybir.dt.uint8
+FP8X4 = mybir.dt.float8_e4m3fn_x4
+SILU = mybir.ActivationFunctionType.Silu
+
+P = 128
+PACK = 4
+CHUNK = 128
+X_LOADS = ((0, 0, 1024, 512), (0, 1024, 2048, 672), (1, 0, 1024, 0), (1, 1024, 1536, 512), (1, 1536, 2048, 336))
+W_VECTOR = ((0, 0), (0, 24), (32, 20))
+W3_LOADS = (((0, 64), (64, 128)), ((0, 64), (64, 128)), ((0, 96), (96, 128)))
+E_LOADS = ((0, 128), (128, 256), (256, 384), (384, 512))
+
+
+def tile_picked_edgeup_silu_e_kernel(tc, xT, eT, w1, w2, w3, w4_words, w4_scales, offs, out):
+    nc = tc.nc
+    with ExitStack() as ctx:
+        sb = ctx.enter_context(tc.tile_pool(name="sb", bufs=1))
+        psum = ctx.enter_context(tc.psum_pool(name="psum", bufs=1))
+
+        def quantise(name, values, tag=None):
+            width = values.shape[1] // PACK
+            codes = sb.tile([P, width], U32, name=name + "_codes", tag=tag or name + "_codes", align_bytes=64)
+            scales = sb.tile([P, width], U8, name=name + "_scales", align_bytes=64)
+            nc.vector.quantize_mx(out=codes[:].bitcast(FP8X4), scales=scales[:], in_=values)
+            return codes, scales
+
+        def product(acc, left, left_cols, right, right_cols, start, stop):
+            nc.tensor.matmul_mx(
+                out=acc,
+                lhsT=left[0][:, left_cols].bitcast(FP8X4),
+                lhsT_scale=left[1][:, left_cols],
+                rhs=right[0][:, right_cols].bitcast(FP8X4),
+                rhs_scale=right[1][:, right_cols],
+                start=start,
+                stop=stop,
+            )
+
+        warm_in = sb.tile([P, 8], F32, name="warm_in")
+        warm_out = sb.tile([P, 8], F32, name="warm_out")
+        nc.vector.memset(warm_in[:], 0.0)
+        nc.scalar.activation(warm_out[:], warm_in[:], SILU)
+
+        w4_codes = sb.tile([P, N], U32, name="w4_codes", align_bytes=64)
+        w4_plane = sb.tile([P, N], U8, name="w4_plane", align_bytes=64)
+        nc.gpsimd.memset(w4_plane[:], 0)
+        for q in range(4):
+            nc.gpsimd.dma_start(out=w4_plane[32 * q : 32 * q + 4, :].bitcast(I32), in_=w4_scales[0, 4 * q : 4 * q + 4, :].bitcast(I32))
+
+        offsets = sb.tile([P, 2 * V // 16], U16, name="offsets")
+        x_rows = xT.rearrange("(p j) c -> p j c", j=PACK)
+        x_raw = []
+        for n, (u, c0, c1, cv) in enumerate(X_LOADS):
+            raw = sb.tile([P, 2, c1 - c0], F32, name="x_raw%d" % n)
+            nc.sync.dma_start(out=raw[:], in_=x_rows[:, 2 * u : 2 * u + 2, c0:c1])
+            x_raw.append(raw)
+            if n == 0:
+                nc.sync.dma_start(offsets[:], offs)
+        w_raw = []
+        for n, w in enumerate((w1, w2, w3)):
+            parts = []
+            for m0, m1 in W3_LOADS[n]:
+                raw = sb.tile([P, PACK, PACK * (m1 - m0)], F32, name="w_raw%d_%d" % (n, m0))
+                nc.sync.dma_start(out=raw[:], in_=w.rearrange("(p j) c -> p j c", j=PACK)[:, :, PACK * m0 : PACK * m1])
+                parts.append((m0, m1, raw))
+            w_raw.append(parts)
+        e_raw = []
+        for c0, c1 in E_LOADS:
+            raw = sb.tile([P, PACK, c1 - c0], F32, name="e_raw%d" % c0)
+            nc.sync.dma_start(out=raw[:], in_=eT.rearrange("(p j) c -> p j c", j=PACK)[:, :, c0:c1])
+            for c in range(c0, c1, CHUNK):
+                e_raw.append(raw[:, :, c - c0 : c - c0 + CHUNK])
+        nc.sync.dma_start(out=w4_codes[:].bitcast(I32), in_=w4_words[0].rearrange("p n t -> p (n t)").bitcast(I32))
+
+        pairs = [sb.tile([P, T], U32, name="pairs%d" % u) for u in range(2)]
+        picked = [sb.tile([P, PACK * V], BF16, name="picked%d" % s, align_bytes=64) for s in range(2)]
+
+        def round_x(n):
+            u, c0, c1, cv = X_LOADS[n]
+            for copy, a, b in ((nc.scalar.copy, cv, c1 - c0), (nc.vector.tensor_copy, 0, cv)):
+                if b > a:
+                    copy(
+                        out=pairs[u][:, c0 + a : c0 + b].bitcast(BF16).rearrange("p (c e) -> p c e", e=2),
+                        in_=x_raw[n][:, :, a:b].rearrange("p e c -> p c e"),
+                    )
+
+        def gather(u, s):
+            nc.vector.tensor_copy(
+                out=picked[s][:].bitcast(U32).rearrange("p (v u) -> p v u", u=2)[:, :, u],
+                in_=pairs[u][:].indirect(offsets[:, s * V // 16 : (s + 1) * V // 16]),
+            )
+
+        w_grouped = [sb.tile([P, PACK * H], BF16, name="w_grouped%d" % n, tag="w_grouped%d" % n, align_bytes=64) for n in range(3)]
+
+        def round_w(n):
+            dealt = w_grouped[n][:].rearrange("p (t m j) -> p m t j", t=PACK, j=PACK)
+            for part, (m0, m1, raw) in enumerate(w_raw[n]):
+                mv = W_VECTOR[n][part]
+                source = raw[:].rearrange("p j (m t) -> p m t j", t=PACK)
+                for copy, a, b in ((nc.scalar.copy, mv, m1 - m0), (nc.vector.tensor_copy, 0, mv)):
+                    if b > a:
+                        copy(out=dealt[:, m0 + a : m0 + b], in_=source[:, a:b])
+
+        acc = [psum.tile([P, PACK, CHUNK], F32, name="acc%d" % c, tag="acc%d" % c) for c in range(V // CHUNK)]
+
+        def node_term(w_q, x_q, first):
+            for c in range(V // CHUNK):
+                for t in range(PACK):
+                    product(acc[c][:, t, :], w_q, slice(t * P, (t + 1) * P), x_q, slice(c * CHUNK, (c + 1) * CHUNK), first and t == 0, False)
+
+        for u in range(2):
+            for n in range(len(X_LOADS)):
+                if X_LOADS[n][0] == u:
+                    round_x(n)
+            gather(u, 0)
+            if u == 0:
+                gather(u, 1)
+        round_w(0)
+        gather(1, 1)
+        src_q = quantise("src", picked[0][:])
+        w1_q = quantise("w1", w_grouped[0][:])
+        node_term(w1_q, src_q, True)
+        dst_q = quantise("dst", picked[1][:], "w_grouped0")
+        round_w(1)
+        w2_q = quantise("w2", w_grouped[1][:])
+        node_term(w2_q, dst_q, False)
+        round_w(2)
+        w3_q = quantise("w3", w_grouped[2][:])
+
+        out_rows = out.rearrange("(a p) v -> p a v", p=P)
+        chunks = V // CHUNK
+        h_values = {}
+
+        def edge_term(c):
+            grouped = sb.tile([P, PACK * CHUNK], BF16, name="e_grouped%d" % c, tag="e_grouped%d" % c, align_bytes=64)
+            (nc.scalar.copy if c < 2 else nc.vector.tensor_copy)(out=grouped[:].rearrange("p (v j) -> p v j", j=PACK), in_=e_raw[c].rearrange("p j v -> p v j"))
+            e_q = quantise("e%d" % c, grouped[:])
+            for t in range(PACK):
+                product(acc[c][:, t, :], w3_q, slice(t * P, (t + 1) * P), e_q, slice(0, CHUNK), False, t == PACK - 1)
+            h = sb.tile([P, PACK * CHUNK], BF16, name="h%d" % c, align_bytes=64)
+            nc.scalar.activation(h[:].rearrange("p (v t) -> p v t", t=PACK), acc[c][:].rearrange("p t v -> p v t"), SILU)
+            h_values[c] = h
+
+        for c in range(chunks):
+            edge_term(c)
+
+        h_codes = sb.tile([P, V], U32, name="h_codes", tag="e_grouped%d" % (chunks - 1), align_bytes=64)
+        h_scales = sb.tile([P, V], U8, name="h_scales", align_bytes=64)
+        for c in range(chunks):
+            cols = slice(c * CHUNK, (c + 1) * CHUNK)
+            nc.vector.quantize_mx(out=h_codes[:, cols].bitcast(FP8X4), scales=h_scales[:, cols], in_=h_values[c][:])
+            staged = sb.tile([P, N // P, CHUNK], F32, name="staged%d" % c)
+            if c < chunks - 1:
+                res = psum.tile([P, N // P, CHUNK], F32, name="res%d" % c)
+                for a in range(N // P):
+                    product(res[:, a, :], (w4_codes, w4_plane), slice(a * P, (a + 1) * P), (h_codes, h_scales), cols, True, True)
+                (nc.vector.tensor_copy, nc.scalar.copy, nc.scalar.copy)[c](out=staged[:], in_=res[:])
+            else:
+                for a, copy in enumerate((nc.scalar.copy, nc.vector.tensor_copy)):
+                    res = psum.tile([P, CHUNK], F32, name="last%d" % a, tag=("acc0", "last")[a])
+                    product(res[:], (w4_codes, w4_plane), slice(a * P, (a + 1) * P), (h_codes, h_scales), cols, True, True)
+                    copy(out=staged[:, a, :], in_=res[:])
+            nc.sync.dma_start(out=out_rows[:, :, cols], in_=staged[:])

@@ -18,7 +18,7 @@ P = 128
 PACK = 4
 CHUNK = 128
 X_LOADS = ((0, 0, 1024, 512), (0, 1024, 2048, 672), (1, 0, 1024, 0), (1, 1024, 1536, 512), (1, 1536, 2048, 336))
-W_VECTOR = ((0, 0), (0, 24), (32, 20))
+W_VECTOR = ((0, 0), (0, 0), (48, 32))
 W3_LOADS = (((0, 64), (64, 128)), ((0, 64), (64, 128)), ((0, 96), (96, 128)))
 E_LOADS = ((0, 128), (128, 256), (256, 384), (384, 512))
 
@@ -55,8 +55,6 @@ def tile_picked_edgeup_silu_e_kernel(tc, xT, eT, w1, w2, w3, w4_words, w4_scales
         w4_codes = sb.tile([P, N], U32, name="w4_codes", align_bytes=64)
         w4_plane = sb.tile([P, N], U8, name="w4_plane", align_bytes=64)
         nc.gpsimd.memset(w4_plane[:], 0)
-        for q in range(4):
-            nc.gpsimd.dma_start(out=w4_plane[32 * q : 32 * q + 4, :].bitcast(I32), in_=w4_scales[0, 4 * q : 4 * q + 4, :].bitcast(I32))
 
         offsets = sb.tile([P, 2 * V // 16], U16, name="offsets")
         x_rows = xT.rearrange("(p j) c -> p j c", j=PACK)
@@ -82,6 +80,8 @@ def tile_picked_edgeup_silu_e_kernel(tc, xT, eT, w1, w2, w3, w4_words, w4_scales
             for c in range(c0, c1, CHUNK):
                 e_raw.append(raw[:, :, c - c0 : c - c0 + CHUNK])
         nc.sync.dma_start(out=w4_codes[:].bitcast(I32), in_=w4_words[0].rearrange("p n t -> p (n t)").bitcast(I32))
+        for q in range(4):
+            nc.sync.dma_start(out=w4_plane[32 * q : 32 * q + 4, :].bitcast(I32), in_=w4_scales[0, 4 * q : 4 * q + 4, :].bitcast(I32))
 
         pairs = [sb.tile([P, T], U32, name="pairs%d" % u) for u in range(2)]
         picked = [sb.tile([P, PACK * V], BF16, name="picked%d" % s, align_bytes=64) for s in range(2)]
@@ -91,8 +91,8 @@ def tile_picked_edgeup_silu_e_kernel(tc, xT, eT, w1, w2, w3, w4_words, w4_scales
             for copy, a, b in ((nc.scalar.copy, cv, c1 - c0), (nc.vector.tensor_copy, 0, cv)):
                 if b > a:
                     copy(
-                        out=pairs[u][:, c0 + a : c0 + b].bitcast(BF16).rearrange("p (c e) -> p c e", e=2),
-                        in_=x_raw[n][:, :, a:b].rearrange("p e c -> p c e"),
+                        out=pairs[u][:, c0 + a : c0 + b].bitcast(BF16).rearrange("p (c i e) -> p c e i", i=4, e=2),
+                        in_=x_raw[n][:, :, a:b].rearrange("p e (c i) -> p c e i", i=4),
                     )
 
         def gather(u, s):
@@ -104,13 +104,15 @@ def tile_picked_edgeup_silu_e_kernel(tc, xT, eT, w1, w2, w3, w4_words, w4_scales
         w_grouped = [sb.tile([P, PACK * H], BF16, name="w_grouped%d" % n, tag="w_grouped%d" % n, align_bytes=64) for n in range(3)]
 
         def round_w(n):
-            dealt = w_grouped[n][:].rearrange("p (t m j) -> p m t j", t=PACK, j=PACK)
+            dealt = w_grouped[n][:].rearrange("p (s r m j) -> p s m j r", s=2, r=2, j=PACK)
             for part, (m0, m1, raw) in enumerate(w_raw[n]):
                 mv = W_VECTOR[n][part]
-                source = raw[:].rearrange("p j (m t) -> p m t j", t=PACK)
-                for copy, a, b in ((nc.scalar.copy, mv, m1 - m0), (nc.vector.tensor_copy, 0, mv)):
-                    if b > a:
-                        copy(out=dealt[:, m0 + a : m0 + b], in_=source[:, a:b])
+                source = raw[:].rearrange("p j (m s r) -> p s m j r", s=2, r=2)
+                if mv < m1 - m0:
+                    nc.scalar.copy(out=dealt[:, :, m0 + mv : m1], in_=source[:, :, mv:])
+                if mv > 0:
+                    for s in range(2):
+                        nc.vector.tensor_copy(out=dealt[:, s, m0 : m0 + mv], in_=source[:, s, :mv])
 
         acc = [psum.tile([P, PACK, CHUNK], F32, name="acc%d" % c, tag="acc%d" % c) for c in range(V // CHUNK)]
 
@@ -144,7 +146,7 @@ def tile_picked_edgeup_silu_e_kernel(tc, xT, eT, w1, w2, w3, w4_words, w4_scales
 
         def edge_term(c):
             grouped = sb.tile([P, PACK * CHUNK], BF16, name="e_grouped%d" % c, tag="e_grouped%d" % c, align_bytes=64)
-            (nc.scalar.copy if c < 2 else nc.vector.tensor_copy)(out=grouped[:].rearrange("p (v j) -> p v j", j=PACK), in_=e_raw[c].rearrange("p j v -> p v j"))
+            (nc.scalar.copy if c < 2 else nc.vector.tensor_copy)(out=grouped[:].rearrange("p (v i j) -> p v j i", i=4, j=PACK), in_=e_raw[c].rearrange("p j (v i) -> p v j i", i=4))
             e_q = quantise("e%d" % c, grouped[:])
             for t in range(PACK):
                 product(acc[c][:, t, :], w3_q, slice(t * P, (t + 1) * P), e_q, slice(0, CHUNK), False, t == PACK - 1)
@@ -155,20 +157,21 @@ def tile_picked_edgeup_silu_e_kernel(tc, xT, eT, w1, w2, w3, w4_words, w4_scales
         for c in range(chunks):
             edge_term(c)
 
-        h_codes = sb.tile([P, V], U32, name="h_codes", tag="e_grouped%d" % (chunks - 1), align_bytes=64)
-        h_scales = sb.tile([P, V], U8, name="h_scales", align_bytes=64)
+        h_scales = sb.tile([P, V], U8, name="h_scales", tag="e_grouped%d" % (chunks - 1), align_bytes=64)
         for c in range(chunks):
             cols = slice(c * CHUNK, (c + 1) * CHUNK)
-            nc.vector.quantize_mx(out=h_codes[:, cols].bitcast(FP8X4), scales=h_scales[:, cols], in_=h_values[c][:])
+            h_codes = sb.tile([P, CHUNK], U32, name="h_codes%d" % c, tag="h_codes%d" % (c % 2), align_bytes=64)
+            nc.vector.quantize_mx(out=h_codes[:].bitcast(FP8X4), scales=h_scales[:, cols], in_=h_values[c][:])
+            h_q = (h_codes[:], h_scales[:, cols])
             staged = sb.tile([P, N // P, CHUNK], F32, name="staged%d" % c)
             if c < chunks - 1:
                 res = psum.tile([P, N // P, CHUNK], F32, name="res%d" % c)
                 for a in range(N // P):
-                    product(res[:, a, :], (w4_codes, w4_plane), slice(a * P, (a + 1) * P), (h_codes, h_scales), cols, True, True)
-                (nc.vector.tensor_copy, nc.scalar.copy, nc.scalar.copy)[c](out=staged[:], in_=res[:])
+                    product(res[:, a, :], (w4_codes, w4_plane), slice(a * P, (a + 1) * P), h_q, slice(0, CHUNK), True, True)
+                (nc.vector.tensor_copy, nc.vector.tensor_copy, nc.scalar.copy)[c](out=staged[:], in_=res[:])
             else:
                 for a, copy in enumerate((nc.scalar.copy, nc.vector.tensor_copy)):
                     res = psum.tile([P, CHUNK], F32, name="last%d" % a, tag=("acc0", "last")[a])
-                    product(res[:], (w4_codes, w4_plane), slice(a * P, (a + 1) * P), (h_codes, h_scales), cols, True, True)
+                    product(res[:], (w4_codes, w4_plane), slice(a * P, (a + 1) * P), h_q, slice(0, CHUNK), True, True)
                     copy(out=staged[:, a, :], in_=res[:])
             nc.sync.dma_start(out=out_rows[:, :, cols], in_=staged[:])

@@ -86,6 +86,14 @@ def tile_picked_edgeup_silu_e_kernel(tc, xT, eT, w1, w2, w3, w4_words, w4_scales
         pairs = [sb.tile([P, T], U32, name="pairs%d" % u) for u in range(2)]
         picked = [sb.tile([P, PACK * V], BF16, name="picked%d" % s, align_bytes=64) for s in range(2)]
 
+        halves = [sb.tile([P, 2 * V], U32, name="halves%d" % s) for s in range(2)]
+
+        def weave(s):
+            nc.vector.tensor_copy(
+                out=picked[s][:].bitcast(I32).rearrange("p (v u) -> p v u", u=2),
+                in_=halves[s][:].bitcast(I32).rearrange("p (u v) -> p v u", u=2),
+            )
+
         def round_x(n):
             u, c0, c1, cv = X_LOADS[n]
             for copy, a, b in ((nc.scalar.copy, cv, c1 - c0), (nc.vector.tensor_copy, 0, cv)):
@@ -97,7 +105,7 @@ def tile_picked_edgeup_silu_e_kernel(tc, xT, eT, w1, w2, w3, w4_words, w4_scales
 
         def gather(u, s):
             nc.vector.tensor_copy(
-                out=picked[s][:].bitcast(U32).rearrange("p (v u) -> p v u", u=2)[:, :, u],
+                out=halves[s][:, u * V : (u + 1) * V],
                 in_=pairs[u][:].indirect(offsets[:, s * V // 16 : (s + 1) * V // 16]),
             )
 
@@ -130,6 +138,8 @@ def tile_picked_edgeup_silu_e_kernel(tc, xT, eT, w1, w2, w3, w4_words, w4_scales
                 gather(u, 1)
         round_w(0)
         gather(1, 1)
+        weave(0)
+        weave(1)
         src_q = quantise("src", picked[0][:])
         w1_q = quantise("w1", w_grouped[0][:])
         node_term(w1_q, src_q, True)

@@ -16,11 +16,13 @@ SILU = mybir.ActivationFunctionType.Silu
 
 P = 128
 PACK = 4
+LINE = 4
 CHUNK = 128
-X_LOADS = ((0, 0, 1024, 512), (0, 1024, 2048, 672), (1, 0, 1024, 0), (1, 1024, 1536, 512), (1, 1536, 2048, 336))
-W_VECTOR = ((0, 0), (0, 0), (48, 32))
-W3_LOADS = (((0, 64), (64, 128)), ((0, 64), (64, 128)), ((0, 96), (96, 128)))
-E_LOADS = ((0, 128), (128, 256), (256, 384), (384, 512))
+CHUNKS = V // CHUNK
+
+X_LOADS = ((0, 0, T, 1360), (1, 0, T // 2, 0), (1, T // 2, T, 672))
+W3_VECTOR_GROUPS = 56
+E_HALF = V // 2
 
 
 def tile_picked_edgeup_silu_e_kernel(tc, xT, eT, w1, w2, w3, w4_words, w4_scales, offs, out):
@@ -36,9 +38,9 @@ def tile_picked_edgeup_silu_e_kernel(tc, xT, eT, w1, w2, w3, w4_words, w4_scales
             nc.vector.quantize_mx(out=codes[:].bitcast(FP8X4), scales=scales[:], in_=values)
             return codes, scales
 
-        def product(acc, left, left_cols, right, right_cols, start, stop):
+        def product(target, left, left_cols, right, right_cols, start, stop):
             nc.tensor.matmul_mx(
-                out=acc,
+                out=target,
                 lhsT=left[0][:, left_cols].bitcast(FP8X4),
                 lhsT_scale=left[1][:, left_cols],
                 rhs=right[0][:, right_cols].bitcast(FP8X4),
@@ -47,19 +49,17 @@ def tile_picked_edgeup_silu_e_kernel(tc, xT, eT, w1, w2, w3, w4_words, w4_scales
                 stop=stop,
             )
 
-        warm_in = sb.tile([P, 8], F32, name="warm_in")
-        warm_out = sb.tile([P, 8], F32, name="warm_out")
-        nc.vector.memset(warm_in[:], 0.0)
-        nc.scalar.activation(warm_out[:], warm_in[:], SILU)
+        def block(n, width):
+            return slice(n * width, (n + 1) * width)
 
         w4_codes = sb.tile([P, N], U32, name="w4_codes", align_bytes=64)
-        w4_plane = sb.tile([P, N], U8, name="w4_plane", align_bytes=64)
-        nc.gpsimd.memset(w4_plane[:], 0)
+        w4_bytes = sb.tile([P, N], U8, name="w4_bytes", align_bytes=64)
+        nc.gpsimd.memset(w4_bytes[:], 0)
 
         offsets = sb.tile([P, 2 * V // 16], U16, name="offsets")
         x_rows = xT.rearrange("(p j) c -> p j c", j=PACK)
         x_raw = []
-        for n, (u, c0, c1, cv) in enumerate(X_LOADS):
+        for n, (u, c0, c1, on_vector) in enumerate(X_LOADS):
             raw = sb.tile([P, 2, c1 - c0], F32, name="x_raw%d" % n)
             nc.sync.dma_start(out=raw[:], in_=x_rows[:, 2 * u : 2 * u + 2, c0:c1])
             x_raw.append(raw)
@@ -67,121 +67,110 @@ def tile_picked_edgeup_silu_e_kernel(tc, xT, eT, w1, w2, w3, w4_words, w4_scales
                 nc.sync.dma_start(offsets[:], offs)
         w_raw = []
         for n, w in enumerate((w1, w2, w3)):
-            parts = []
-            for m0, m1 in W3_LOADS[n]:
-                raw = sb.tile([P, PACK, PACK * (m1 - m0)], F32, name="w_raw%d_%d" % (n, m0))
-                nc.sync.dma_start(out=raw[:], in_=w.rearrange("(p j) c -> p j c", j=PACK)[:, :, PACK * m0 : PACK * m1])
-                parts.append((m0, m1, raw))
-            w_raw.append(parts)
+            raw = sb.tile([P, PACK, H], F32, name="w_raw%d" % n)
+            nc.sync.dma_start(out=raw[:], in_=w.rearrange("(p j) c -> p j c", j=PACK))
+            w_raw.append(raw)
         e_raw = []
-        for c0, c1 in E_LOADS:
-            raw = sb.tile([P, PACK, c1 - c0], F32, name="e_raw%d" % c0)
-            nc.sync.dma_start(out=raw[:], in_=eT.rearrange("(p j) c -> p j c", j=PACK)[:, :, c0:c1])
-            for c in range(c0, c1, CHUNK):
-                e_raw.append(raw[:, :, c - c0 : c - c0 + CHUNK])
+        for half in range(V // E_HALF):
+            raw = sb.tile([P, PACK, E_HALF], F32, name="e_raw%d" % half)
+            nc.sync.dma_start(out=raw[:], in_=eT.rearrange("(p j) c -> p j c", j=PACK)[:, :, block(half, E_HALF)])
+            e_raw.extend(raw[:, :, block(n, CHUNK)] for n in range(E_HALF // CHUNK))
         nc.sync.dma_start(out=w4_codes[:].bitcast(I32), in_=w4_words[0].rearrange("p n t -> p (n t)").bitcast(I32))
         for q in range(4):
-            nc.sync.dma_start(out=w4_plane[32 * q : 32 * q + 4, :].bitcast(I32), in_=w4_scales[0, 4 * q : 4 * q + 4, :].bitcast(I32))
+            nc.sync.dma_start(out=w4_bytes[32 * q : 32 * q + 4, :].bitcast(I32), in_=w4_scales[0, 4 * q : 4 * q + 4, :].bitcast(I32))
 
         pairs = [sb.tile([P, T], U32, name="pairs%d" % u) for u in range(2)]
-        picked = [sb.tile([P, PACK * V], BF16, name="picked%d" % s, align_bytes=64) for s in range(2)]
-
-        halves = [sb.tile([P, 2 * V], U32, name="halves%d" % s) for s in range(2)]
-
-        def weave(s):
-            nc.vector.tensor_copy(
-                out=picked[s][:].bitcast(I32).rearrange("p (v u) -> p v u", u=2),
-                in_=halves[s][:].bitcast(I32).rearrange("p (u v) -> p v u", u=2),
-            )
+        picked = [sb.tile([P, PACK * V], BF16, name="picked%d" % side, align_bytes=64) for side in range(2)]
+        gathered = [sb.tile([P, 2 * V], U32, name="gathered%d" % side) for side in range(2)]
 
         def round_x(n):
-            u, c0, c1, cv = X_LOADS[n]
-            for copy, a, b in ((nc.scalar.copy, cv, c1 - c0), (nc.vector.tensor_copy, 0, cv)):
+            u, c0, c1, on_vector = X_LOADS[n]
+            for copy, a, b in ((nc.scalar.copy, on_vector, c1 - c0), (nc.vector.tensor_copy, 0, on_vector)):
                 if b > a:
                     copy(
-                        out=pairs[u][:, c0 + a : c0 + b].bitcast(BF16).rearrange("p (c i e) -> p c e i", i=4, e=2),
-                        in_=x_raw[n][:, :, a:b].rearrange("p e (c i) -> p c e i", i=4),
+                        out=pairs[u][:, c0 + a : c0 + b].bitcast(BF16).rearrange("p (c i e) -> p c e i", i=LINE, e=2),
+                        in_=x_raw[n][:, :, a:b].rearrange("p e (c i) -> p c e i", i=LINE),
                     )
 
-        def gather(u, s):
+        def gather(u, side):
+            nc.vector.tensor_copy(out=gathered[side][:, block(u, V)], in_=pairs[u][:].indirect(offsets[:, block(side, V // 16)]))
+
+        def weave(side):
             nc.vector.tensor_copy(
-                out=halves[s][:, u * V : (u + 1) * V],
-                in_=pairs[u][:].indirect(offsets[:, s * V // 16 : (s + 1) * V // 16]),
+                out=picked[side][:].bitcast(I32).rearrange("p (v u) -> p v u", u=2),
+                in_=gathered[side][:].bitcast(I32).rearrange("p (u v) -> p v u", u=2),
             )
 
-        w_grouped = [sb.tile([P, PACK * H], BF16, name="w_grouped%d" % n, tag="w_grouped%d" % n, align_bytes=64) for n in range(3)]
+        w_dealt = [sb.tile([P, PACK * H], BF16, name="w_dealt%d" % n, tag="w_dealt%d" % n, align_bytes=64) for n in range(3)]
 
-        def round_w(n):
-            dealt = w_grouped[n][:].rearrange("p (s r m j) -> p s m j r", s=2, r=2, j=PACK)
-            for part, (m0, m1, raw) in enumerate(w_raw[n]):
-                mv = W_VECTOR[n][part]
-                source = raw[:].rearrange("p j (m s r) -> p s m j r", s=2, r=2)
-                if mv < m1 - m0:
-                    nc.scalar.copy(out=dealt[:, :, m0 + mv : m1], in_=source[:, :, mv:])
-                if mv > 0:
-                    for s in range(2):
-                        nc.vector.tensor_copy(out=dealt[:, s, m0 : m0 + mv], in_=source[:, s, :mv])
+        def round_w(n, on_vector):
+            dealt = w_dealt[n][:].rearrange("p (s r m j) -> p s m j r", s=2, r=2, j=PACK)
+            source = w_raw[n][:].rearrange("p j (m s r) -> p s m j r", s=2, r=2)
+            nc.scalar.copy(out=dealt[:, :, on_vector:], in_=source[:, :, on_vector:])
+            if on_vector > 0:
+                for s in range(2):
+                    nc.vector.tensor_copy(out=dealt[:, s, :on_vector], in_=source[:, s, :on_vector])
 
-        acc = [psum.tile([P, PACK, CHUNK], F32, name="acc%d" % c, tag="acc%d" % c) for c in range(V // CHUNK)]
+        acc = [psum.tile([P, PACK, CHUNK], F32, name="acc%d" % c, tag="acc%d" % c) for c in range(CHUNKS)]
 
-        def node_term(w_q, x_q, first):
-            for c in range(V // CHUNK):
+        def node_term(w_q, x_q, first_term):
+            for c in range(CHUNKS):
                 for t in range(PACK):
-                    product(acc[c][:, t, :], w_q, slice(t * P, (t + 1) * P), x_q, slice(c * CHUNK, (c + 1) * CHUNK), first and t == 0, False)
+                    product(acc[c][:, t, :], w_q, block(t, P), x_q, block(c, CHUNK), first_term and t == 0, False)
 
-        for u in range(2):
-            for n in range(len(X_LOADS)):
-                if X_LOADS[n][0] == u:
-                    round_x(n)
-            gather(u, 0)
-            if u == 0:
-                gather(u, 1)
-        round_w(0)
+        round_x(0)
+        gather(0, 0)
+        gather(0, 1)
+        round_x(1)
+        round_x(2)
+        gather(1, 0)
+        round_w(0, 0)
         gather(1, 1)
         weave(0)
         weave(1)
         src_q = quantise("src", picked[0][:])
-        w1_q = quantise("w1", w_grouped[0][:])
+        w1_q = quantise("w1", w_dealt[0][:])
         node_term(w1_q, src_q, True)
-        dst_q = quantise("dst", picked[1][:], "w_grouped0")
-        round_w(1)
-        w2_q = quantise("w2", w_grouped[1][:])
+        dst_q = quantise("dst", picked[1][:], "w_dealt0")
+        round_w(1, 0)
+        w2_q = quantise("w2", w_dealt[1][:])
         node_term(w2_q, dst_q, False)
-        round_w(2)
-        w3_q = quantise("w3", w_grouped[2][:])
+        round_w(2, W3_VECTOR_GROUPS)
+        w3_q = quantise("w3", w_dealt[2][:])
 
-        out_rows = out.rearrange("(a p) v -> p a v", p=P)
-        chunks = V // CHUNK
-        h_values = {}
-
-        def edge_term(c):
-            grouped = sb.tile([P, PACK * CHUNK], BF16, name="e_grouped%d" % c, tag="e_grouped%d" % c, align_bytes=64)
-            (nc.scalar.copy if c < 2 else nc.vector.tensor_copy)(out=grouped[:].rearrange("p (v i j) -> p v j i", i=4, j=PACK), in_=e_raw[c].rearrange("p j (v i) -> p v j i", i=4))
-            e_q = quantise("e%d" % c, grouped[:])
+        h_values = []
+        for c in range(CHUNKS):
+            e_values = sb.tile([P, PACK * CHUNK], BF16, name="e_values%d" % c, tag="e_values%d" % c, align_bytes=64)
+            copy = nc.scalar.copy if c * CHUNK < E_HALF else nc.vector.tensor_copy
+            copy(
+                out=e_values[:].rearrange("p (v i j) -> p v j i", i=LINE, j=PACK),
+                in_=e_raw[c].rearrange("p j (v i) -> p v j i", i=LINE),
+            )
+            e_q = quantise("e%d" % c, e_values[:])
             for t in range(PACK):
-                product(acc[c][:, t, :], w3_q, slice(t * P, (t + 1) * P), e_q, slice(0, CHUNK), False, t == PACK - 1)
+                product(acc[c][:, t, :], w3_q, block(t, P), e_q, block(0, CHUNK), False, t == PACK - 1)
             h = sb.tile([P, PACK * CHUNK], BF16, name="h%d" % c, align_bytes=64)
             nc.scalar.activation(h[:].rearrange("p (v t) -> p v t", t=PACK), acc[c][:].rearrange("p t v -> p v t"), SILU)
-            h_values[c] = h
+            h_values.append(h)
 
-        for c in range(chunks):
-            edge_term(c)
-
-        h_scales = sb.tile([P, V], U8, name="h_scales", tag="e_grouped%d" % (chunks - 1), align_bytes=64)
-        for c in range(chunks):
-            cols = slice(c * CHUNK, (c + 1) * CHUNK)
+        w4_q = (w4_codes, w4_bytes)
+        out_rows = out.rearrange("(a p) v -> p a v", p=P)
+        h_scales = sb.tile([P, V], U8, name="h_scales", tag="e_values%d" % (CHUNKS - 1), align_bytes=64)
+        for c in range(CHUNKS):
+            cols = block(c, CHUNK)
             h_codes = sb.tile([P, CHUNK], U32, name="h_codes%d" % c, tag="h_codes%d" % (c % 2), align_bytes=64)
             nc.vector.quantize_mx(out=h_codes[:].bitcast(FP8X4), scales=h_scales[:, cols], in_=h_values[c][:])
             h_q = (h_codes[:], h_scales[:, cols])
             staged = sb.tile([P, N // P, CHUNK], F32, name="staged%d" % c)
-            if c < chunks - 1:
+            if c < CHUNKS - 1:
                 res = psum.tile([P, N // P, CHUNK], F32, name="res%d" % c)
                 for a in range(N // P):
-                    product(res[:, a, :], (w4_codes, w4_plane), slice(a * P, (a + 1) * P), h_q, slice(0, CHUNK), True, True)
-                (nc.vector.tensor_copy, nc.vector.tensor_copy, nc.scalar.copy)[c](out=staged[:], in_=res[:])
+                    product(res[:, a, :], w4_q, block(a, P), h_q, block(0, CHUNK), True, True)
+                copy = nc.scalar.copy if c == CHUNKS - 2 else nc.vector.tensor_copy
+                copy(out=staged[:], in_=res[:])
             else:
                 for a, copy in enumerate((nc.scalar.copy, nc.vector.tensor_copy)):
                     res = psum.tile([P, CHUNK], F32, name="last%d" % a, tag=("acc0", "last")[a])
-                    product(res[:], (w4_codes, w4_plane), slice(a * P, (a + 1) * P), h_q, slice(0, CHUNK), True, True)
+                    product(res[:], w4_q, block(a, P), h_q, block(0, CHUNK), True, True)
                     copy(out=staged[:, a, :], in_=res[:])
             nc.sync.dma_start(out=out_rows[:, :, cols], in_=staged[:])

@@ -52,6 +52,11 @@ def tile_picked_edgeup_silu_e_kernel(tc, xT, eT, w1, w2, w3, w4_words, w4_scales
         def block(n, width):
             return slice(n * width, (n + 1) * width)
 
+        warm_in = sb.tile([P, 8], F32, name="warm_in")
+        warm_out = sb.tile([P, 8], F32, name="warm_out")
+        nc.vector.memset(warm_in[:], 0.0)
+        nc.scalar.activation(warm_out[:], warm_in[:], SILU)
+
         w4_codes = sb.tile([P, N], U32, name="w4_codes", align_bytes=64)
         w4_bytes = sb.tile([P, N], U8, name="w4_bytes", align_bytes=64)
         nc.gpsimd.memset(w4_bytes[:], 0)

from contextlib import ExitStack

import concourse.mybir as mybir

K, T, V, H, N = 512, 2048, 512, 512, 256
FLOPS = 2 * V * H * (3 * K + N)

F32 = mybir.dt.float32
BF16 = mybir.dt.bfloat16
I32 = mybir.dt.int32
U32 = mybir.dt.uint32
U16 = mybir.dt.uint16
U8 = mybir.dt.uint8
FP8X4 = mybir.dt.float8_e4m3fn_x4
SILU = mybir.ActivationFunctionType.Silu

P = 128
PACK = 4
LINE = 4
CHUNK = 128
CHUNKS = V // CHUNK

X_LOADS = ((0, 0, T, 1360), (1, 0, T // 2, 0), (1, T // 2, T, 672))
W3_VECTOR_GROUPS = 56
E_HALF = V // 2


def tile_picked_edgeup_silu_e_kernel(tc, xT, eT, w1, w2, w3, w4_words, w4_scales, offs, out):
    nc = tc.nc
    with ExitStack() as ctx:
        sb = ctx.enter_context(tc.tile_pool(name="sb", bufs=1))
        psum = ctx.enter_context(tc.psum_pool(name="psum", bufs=1))

        def quantise(name, values, tag=None):
            width = values.shape[1] // PACK
            codes = sb.tile([P, width], U32, name=name + "_codes", tag=tag or name + "_codes", align_bytes=64)
            scales = sb.tile([P, width], U8, name=name + "_scales", align_bytes=64)
            nc.vector.quantize_mx(out=codes[:].bitcast(FP8X4), scales=scales[:], in_=values)
            return codes, scales

        def product(target, left, left_cols, right, right_cols, start, stop):
            nc.tensor.matmul_mx(
                out=target,
                lhsT=left[0][:, left_cols].bitcast(FP8X4),
                lhsT_scale=left[1][:, left_cols],
                rhs=right[0][:, right_cols].bitcast(FP8X4),
                rhs_scale=right[1][:, right_cols],
                start=start,
                stop=stop,
            )

        def block(n, width):
            return slice(n * width, (n + 1) * width)

        warm_in = sb.tile([P, 8], F32, name="warm_in")
        warm_out = sb.tile([P, 8], F32, name="warm_out")
        nc.vector.memset(warm_in[:], 0.0)
        nc.scalar.activation(warm_out[:], warm_in[:], SILU)

        w4_codes = sb.tile([P, N], U32, name="w4_codes", align_bytes=64)
        w4_bytes = sb.tile([P, N], U8, name="w4_bytes", align_bytes=64)
        nc.gpsimd.memset(w4_bytes[:], 0)

        offsets = sb.tile([P, 2 * V // 16], U16, name="offsets")
        x_rows = xT.rearrange("(p j) c -> p j c", j=PACK)
        x_raw = []
        for n, (u, c0, c1, on_vector) in enumerate(X_LOADS):
            raw = sb.tile([P, 2, c1 - c0], F32, name="x_raw%d" % n)
            nc.sync.dma_start(out=raw[:], in_=x_rows[:, 2 * u : 2 * u + 2, c0:c1])
            x_raw.append(raw)
            if n == 0:
                nc.sync.dma_start(offsets[:], offs)
        w_raw = []
        for n, w in enumerate((w1, w2, w3)):
            raw = sb.tile([P, PACK, H], F32, name="w_raw%d" % n)
            nc.sync.dma_start(out=raw[:], in_=w.rearrange("(p j) c -> p j c", j=PACK))
            w_raw.append(raw)
        e_raw = []
        for half in range(V // E_HALF):
            raw = sb.tile([P, PACK, E_HALF], F32, name="e_raw%d" % half)
            nc.sync.dma_start(out=raw[:], in_=eT.rearrange("(p j) c -> p j c", j=PACK)[:, :, block(half, E_HALF)])
            e_raw.extend(raw[:, :, block(n, CHUNK)] for n in range(E_HALF // CHUNK))
        nc.sync.dma_start(out=w4_codes[:].bitcast(I32), in_=w4_words[0].rearrange("p n t -> p (n t)").bitcast(I32))
        for q in range(4):
            nc.sync.dma_start(out=w4_bytes[32 * q : 32 * q + 4, :].bitcast(I32), in_=w4_scales[0, 4 * q : 4 * q + 4, :].bitcast(I32))

        pairs = [sb.tile([P, T], U32, name="pairs%d" % u) for u in range(2)]
        picked = [sb.tile([P, PACK * V], BF16, name="picked%d" % side, align_bytes=64) for side in range(2)]
        gathered = [sb.tile([P, 2 * V], U32, name="gathered%d" % side) for side in range(2)]

        def round_x(n):
            u, c0, c1, on_vector = X_LOADS[n]
            for copy, a, b in ((nc.scalar.copy, on_vector, c1 - c0), (nc.vector.tensor_copy, 0, on_vector)):
                if b > a:
                    copy(
                        out=pairs[u][:, c0 + a : c0 + b].bitcast(BF16).rearrange("p (c i e) -> p c e i", i=LINE, e=2),
                        in_=x_raw[n][:, :, a:b].rearrange("p e (c i) -> p c e i", i=LINE),
                    )

        def gather(u, side):
            nc.vector.tensor_copy(out=gathered[side][:, block(u, V)], in_=pairs[u][:].indirect(offsets[:, block(side, V // 16)]))

        def weave(side):
            nc.vector.tensor_copy(
                out=picked[side][:].bitcast(I32).rearrange("p (v u) -> p v u", u=2),
                in_=gathered[side][:].bitcast(I32).rearrange("p (u v) -> p v u", u=2),
            )

        w_dealt = [sb.tile([P, PACK * H], BF16, name="w_dealt%d" % n, tag="w_dealt%d" % n, align_bytes=64) for n in range(3)]

        def round_w(n, on_vector):
            dealt = w_dealt[n][:].rearrange("p (s r m j) -> p s m j r", s=2, r=2, j=PACK)
            source = w_raw[n][:].rearrange("p j (m s r) -> p s m j r", s=2, r=2)
            nc.scalar.copy(out=dealt[:, :, on_vector:], in_=source[:, :, on_vector:])
            if on_vector > 0:
                for s in range(2):
                    nc.vector.tensor_copy(out=dealt[:, s, :on_vector], in_=source[:, s, :on_vector])

        acc = [psum.tile([P, PACK, CHUNK], F32, name="acc%d" % c, tag="acc%d" % c) for c in range(CHUNKS)]

        def node_term(w_q, x_q, first_term):
            for c in range(CHUNKS):
                for t in range(PACK):
                    product(acc[c][:, t, :], w_q, block(t, P), x_q, block(c, CHUNK), first_term and t == 0, False)

        round_x(0)
        gather(0, 0)
        gather(0, 1)
        round_x(1)
        round_x(2)
        gather(1, 0)
        round_w(0, 0)
        gather(1, 1)
        weave(0)
        weave(1)
        src_q = quantise("src", picked[0][:])
        w1_q = quantise("w1", w_dealt[0][:])
        node_term(w1_q, src_q, True)
        dst_q = quantise("dst", picked[1][:], "w_dealt0")
        round_w(1, 0)
        w2_q = quantise("w2", w_dealt[1][:])
        node_term(w2_q, dst_q, False)
        round_w(2, W3_VECTOR_GROUPS)
        w3_q = quantise("w3", w_dealt[2][:])

        h_values = []
        for c in range(CHUNKS):
            e_values = sb.tile([P, PACK * CHUNK], BF16, name="e_values%d" % c, tag="e_values%d" % c, align_bytes=64)
            copy = nc.scalar.copy if c * CHUNK < E_HALF else nc.vector.tensor_copy
            copy(
                out=e_values[:].rearrange("p (v i j) -> p v j i", i=LINE, j=PACK),
                in_=e_raw[c].rearrange("p j (v i) -> p v j i", i=LINE),
            )
            e_q = quantise("e%d" % c, e_values[:])
            for t in range(PACK):
                product(acc[c][:, t, :], w3_q, block(t, P), e_q, block(0, CHUNK), False, t == PACK - 1)
            h = sb.tile([P, PACK * CHUNK], BF16, name="h%d" % c, align_bytes=64)
            nc.scalar.activation(h[:].rearrange("p (v t) -> p v t", t=PACK), acc[c][:].rearrange("p t v -> p v t"), SILU)
            h_values.append(h)

        w4_q = (w4_codes, w4_bytes)
        out_rows = out.rearrange("(a p) v -> p a v", p=P)
        h_scales = sb.tile([P, V], U8, name="h_scales", tag="e_values%d" % (CHUNKS - 1), align_bytes=64)
        for c in range(CHUNKS):
            cols = block(c, CHUNK)
            h_codes = sb.tile([P, CHUNK], U32, name="h_codes%d" % c, tag="h_codes%d" % (c % 2), align_bytes=64)
            nc.vector.quantize_mx(out=h_codes[:].bitcast(FP8X4), scales=h_scales[:, cols], in_=h_values[c][:])
            h_q = (h_codes[:], h_scales[:, cols])
            staged = sb.tile([P, N // P, CHUNK], F32, name="staged%d" % c)
            if c < CHUNKS - 1:
                res = psum.tile([P, N // P, CHUNK], F32, name="res%d" % c)
                for a in range(N // P):
                    product(res[:, a, :], w4_q, block(a, P), h_q, block(0, CHUNK), True, True)
                copy = nc.scalar.copy if c == CHUNKS - 2 else nc.vector.tensor_copy
                copy(out=staged[:], in_=res[:])
            else:
                for a, copy in enumerate((nc.scalar.copy, nc.vector.tensor_copy)):
                    res = psum.tile([P, CHUNK], F32, name="last%d" % a, tag=("acc0", "last")[a])
                    product(res[:], w4_q, block(a, P), h_q, block(0, CHUNK), True, True)
                    copy(out=staged[:, a, :], in_=res[:])
            nc.sync.dma_start(out=out_rows[:, :, cols], in_=staged[:])
